import numpy as np
import ml_dtypes


def mxq(x, axis, fmt="e4m3"):
    dtype, down = {"e4m3": (ml_dtypes.float8_e4m3fn, 7), "e5m2": (ml_dtypes.float8_e5m2, 14)}[fmt]
    v = np.moveaxis(np.asarray(x, np.float32).astype(ml_dtypes.bfloat16).astype(np.float64), axis, -1)
    blocks = v.reshape(v.shape[:-1] + (-1, 32))
    amax = np.abs(blocks).max(-1, keepdims=True)
    byte = np.maximum(np.where(amax > 0, np.frexp(amax)[1] - 1 + 127, 0) - down, 1)
    scale = np.exp2(byte - 127.0)
    codes = (blocks / scale).astype(np.float32).astype(dtype).astype(np.float64)
    return np.moveaxis((codes * scale).reshape(v.shape), -1, axis)


WIDE = False


def mx_kscale(k):
    if not WIDE:
        return np.ones(k)
    levels = np.array([10, -10, 5, -5, 0])
    if k % 512:
        return np.exp2(np.random.permutation(np.resize(levels, k // 32))).repeat(32)
    a = np.empty((k // 512, 16))
    for p in range(k // 512):
        a[p, :8] = np.random.permutation(np.resize(levels, 8))
        for g in range(8):
            far = levels[np.abs(levels - a[p, g]) >= 10]
            a[p, g + 8] = far[np.random.randint(len(far))]
    return np.exp2(a.ravel()).repeat(32)


BF16 = ml_dtypes.bfloat16


def bf(x):
    return np.asarray(x, np.float32).astype(BF16)


def f64(x):
    return np.asarray(x).astype(np.float64)

def planes(Y):
    n, m = Y.shape
    b = f64(bf(Y)).reshape(n // 32, 32, m)
    amax = np.abs(b).max(1)
    byte = np.clip(np.where(amax > 0, np.frexp(amax)[1] - 1 + 127 - 7, 1), 1, 254)
    codes = (b * np.exp2(127.0 - byte)[:, None, :]).reshape(n, m).astype(np.float32).astype(ml_dtypes.float8_e4m3fn).view(np.uint8)
    words = codes.reshape(n // 512, 128, 4, m).transpose(0, 1, 3, 2)
    return np.ascontiguousarray(words), np.ascontiguousarray(byte.astype(np.uint8).reshape(n // 512, 16, m))


H, SQ, SK, D = 4, 512, 512, 512
CAP = 6.0


def sink_softmax(s, sink):
    sink_b = sink[:, None, None]
    m = np.maximum(np.max(s, axis=-1, keepdims=True), sink_b)
    ex = np.exp(s - m)
    return ex / (np.sum(ex, axis=-1, keepdims=True) + np.exp(sink_b - m))


def setup_inputs():
    c = mx_kscale(D)
    t = mx_kscale(D)
    u = mx_kscale(SQ)
    return {
        "q": bf(np.random.standard_normal((H, SQ, D)) * 2.0 * c[None, None, :] * u[None, :, None]),
        "k": bf(np.random.standard_normal((H, SK, D))),
        "v": bf(np.random.standard_normal((H, SK, D)) / t[None, None, :]),
        "d_o": bf(np.random.standard_normal((H, SQ, D)) * t[None, None, :]),
        "sink": bf(6.0 + 0.5 * np.random.standard_normal(H)),
        "tau": bf((1.0 + 0.1 * np.random.standard_normal((H, SQ))) / u[None, :]),
        "a": bf((1.0 + 0.1 * np.random.standard_normal((H, D))) / c[None, :]),
    }


def core(q, k, v, d_o, sink, tau, a):
    q, k, v, d_o = f64(q), f64(k), f64(v), f64(d_o)
    sink, tau, a = f64(sink), f64(tau), f64(a)
    root_d = np.sqrt(D)

    ka = k * a[:, None, :]

    qk = mxq(q, 2, "e4m3") @ mxq(ka, 2, "e4m3").transpose(0, 2, 1)
    z = tau[:, :, None] * qk / root_d

    s = CAP * np.tanh(z / CAP)

    p = sink_softmax(s, sink)

    dp = mxq(d_o, 2, "e4m3") @ mxq(v, 2, "e4m3").transpose(0, 2, 1)

    delta = np.sum(p * dp, axis=-1, keepdims=True)
    dz = p * (dp - delta) * (1.0 - (s / CAP) ** 2)

    g = tau[:, :, None] * dz

    gq = mxq(g, 1, "e4m3").transpose(0, 2, 1) @ mxq(q, 1, "e4m3")
    return a[:, None, :] * gq / root_d


def reference(q, k, v, d_o, sink, tau, a):
    R_out = core(q, k, v, d_o, sink, tau, a)
    words, scales = planes(np.moveaxis(R_out, 2, 0).reshape(512, -1))
    return R_out, words, scales

@@ -1,0 +1,417 @@
+import math
+from contextlib import ExitStack
+
+import concourse.mybir as mybir
+from concourse.masks import make_identity
+
+H, S, D = 4, 512, 512
+CAP = 6.0
+FLOPS = 3 * 2 * H * S * S * D
+
+F32 = mybir.dt.float32
+BF16 = mybir.dt.bfloat16
+I32 = mybir.dt.int32
+U32 = mybir.dt.uint32
+U8 = mybir.dt.uint8
+FP8X4 = mybir.dt.float8_e4m3fn_x4
+ALU = mybir.AluOpType
+ACT = mybir.ActivationFunctionType
+
+P = 128
+PACK = 4
+W = 512
+
+
+def tile_softcapsinkattentionbackward_x1_kernel(tc, q, k, v, d_o, sink, tau, a, out_0, out_1, out_2):
+    nc = tc.nc
+    inv_root_d = 1.0 / math.sqrt(D)
+    with ExitStack() as ctx:
+        sb = ctx.enter_context(tc.tile_pool(name="sb", bufs=1))
+        ps = ctx.enter_context(tc.psum_pool(name="ps", bufs=1))
+        ctx.enter_context(tc.manual_schedule())
+
+        def tiles(name, count, shape, dtype):
+            return [sb.tile(shape, dtype, name="%s%d" % (name, n), align_bytes=64) for n in range(count)]
+
+        rows = {name: tiles(name, H, [P, PACK, D], BF16) for name in ("q", "k", "v", "do")}
+        names = ("qd", "kd", "dod", "vd", "qi", "gi")
+        stage = {name: sb.tile([P, W * PACK], BF16, name="stage_" + name, align_bytes=64) for name in names + ("od",)}
+        codes = {name: tiles("codes_" + name, 2, [P, W], U32) for name in names}
+        scales = {name: tiles("scales_" + name, 2, [P, W], U8) for name in names}
+        out_codes = sb.tile([P, H, W], U32, align_bytes=64)
+        out_scales = sb.tile([P, H * W], U8, align_bytes=64)
+        th = tiles("th", 2, [P, PACK, S], F32)
+        ex = tiles("ex", 2, [P, PACK, S], F32)
+        grad = sb.tile([P, PACK, S], F32, align_bytes=64)
+        res = tiles("res", 2, [P, PACK, D], F32)
+        res16 = sb.tile([P, PACK, D], BF16, align_bytes=64)
+        banks = [ps.tile([P, W], F32, name="bank%d" % n) for n in range(8)]
+        turn = {"vector": [], "scalar": []}
+
+        def next_bank(reader):
+            turn[reader].append(0)
+            first = 0 if reader == "vector" else 4
+            return banks[first + (len(turn[reader]) - 1) % 4]
+
+        a_part = sb.tile([P, H, PACK], BF16)
+        tau16 = sb.tile([P, H, PACK], BF16)
+        sink16 = sb.tile([P, H], BF16)
+        a_free = sb.tile([P, H, D], BF16)
+        tau32 = sb.tile([P, H, PACK], F32)
+        z_scale = sb.tile([P, H, PACK], F32)
+        neg_max = sb.tile([P, H], F32)
+        sink_gap = sb.tile([P, H], F32)
+        sink_exp = sb.tile([P, H], F32)
+        ex_sum = tiles("ex_sum", H, [P, PACK], F32)
+        denom = tiles("denom", H, [P, PACK], F32)
+        inv_denom = tiles("inv_denom", H, [P, PACK], F32)
+        gain = tiles("gain", H, [P, PACK], F32)
+        dot = tiles("dot", H, [P, PACK], F32)
+        shift = tiles("shift", H, [P, PACK], F32)
+        ident32 = sb.tile([P, P], F32)
+        ident16 = sb.tile([P, P], BF16)
+
+        def load(name, src, h, slots=slice(0, PACK)):
+            pattern = "(p t) d -> p t d" if name in ("q", "do") else "(t p) d -> p t d"
+            view = src[h].rearrange(pattern, t=PACK)
+            nc.sync.dma_start(out=rows[name][h][:, slots, :], in_=view[:, slots, :])
+
+        pending = {}
+
+        def turn_block(h, b):
+            bank = next_bank("scalar")
+            words = res16[:, b, :].bitcast(F32)
+            for u in range(2):
+                nc.tensor.transpose(bank[:, u * P : (u + 1) * P], words[:, u : 2 * P : 2], ident32[:])
+            pending[("od", h), b] = bank
+
+        def take_block(h, b):
+            nc.scalar.copy(
+                out=stage["od"][:, b * W : (b + 1) * W].bitcast(F32).rearrange("p (c u) -> p c u", u=2),
+                in_=pending[("od", h), b][:, : 2 * P].rearrange("p (u c) -> p c u", u=2),
+            )
+
+        def turn_rows(key, src, half, reader):
+            bank = next_bank(reader)
+            view = bank[:].rearrange("p (u s r) -> p u s r", u=2, s=2)
+            for s in range(2):
+                words = src[:, 2 * half + s, :].bitcast(F32)
+                for u in range(2):
+                    nc.tensor.transpose(view[:, u, s, :], words[:, u : 2 * P : 2], ident32[:])
+            pending[key, half] = bank
+
+        def half_of(name, half):
+            return stage[name][:, half * 1024 : (half + 1) * 1024]
+
+        def take_turned(key, half, engine):
+            bank = pending[key, half]
+            dst = half_of(key[0], half).bitcast(F32).rearrange("p (c u) -> p c u", u=2)
+            src = bank[:].rearrange("p (u c) -> p c u", u=2)
+            if engine == "scalar":
+                nc.scalar.copy(out=dst, in_=src)
+            else:
+                nc.vector.tensor_copy(out=dst, in_=src)
+
+        def take_gained_keys(h, half):
+            bank = pending[("kd", h), half]
+            nc.vector.tensor_tensor(
+                out=half_of("kd", half).rearrange("p (c u e) -> p c u e", u=2, e=2),
+                in0=bank[:].bitcast(BF16).rearrange("p (u c e) -> p c u e", u=2, e=2),
+                in1=a_part[:, h, :].rearrange("p (u e) -> p u e", u=2).unsqueeze(1).to_broadcast([P, 256, 2, 2]),
+                op=ALU.mult,
+            )
+
+        def quantise(name, h, part=0, parts=1):
+            n = W // parts
+            cols = slice(part * n, (part + 1) * n)
+            if name == "od":
+                c, s = out_codes[:, h, cols], out_scales[:, h * W + part * n : h * W + (part + 1) * n]
+            else:
+                c, s = codes[name][h % 2][:, cols], scales[name][h % 2][:, cols]
+            nc.vector.quantize_mx(out=c.bitcast(FP8X4), scales=s, in_=stage[name][:, PACK * part * n : PACK * (part + 1) * n])
+
+        def product(key, h, block, still, moving, reader):
+            bank = next_bank(reader)
+            cols = slice(block * P, (block + 1) * P)
+            nc.tensor.matmul_mx(
+                out=bank[:],
+                lhsT=codes[still][h % 2][:, cols].bitcast(FP8X4),
+                lhsT_scale=scales[still][h % 2][:, cols],
+                rhs=codes[moving][h % 2][:].bitcast(FP8X4),
+                rhs_scale=scales[moving][h % 2][:],
+                start=True,
+                stop=True,
+            )
+            pending[(key, h), block] = bank
+
+        def weave_q(h, half):
+            bank = next_bank("scalar")
+            wide = bank[:].bitcast(BF16)
+            for c in range(2):
+                d0 = (2 * half + c) * P
+                nc.tensor.matmul(
+                    out=wide[:, c * W : (c + 1) * W],
+                    lhsT=ident16[:],
+                    rhs=rows["q"][h][:, :, d0 : d0 + P].rearrange("p t d -> p d t"),
+                    start=True,
+                    stop=True,
+                )
+            pending[("qi", h), half] = bank
+
+        def take_woven(h, half):
+            nc.scalar.copy(out=half_of("qi", half), in_=pending[("qi", h), half][:].bitcast(BF16))
+
+        def softcap(h, t):
+            nc.scalar.activation(out=th[h % 2][:, t, :], in_=pending[("z", h), t][:], func=ACT.Tanh, scale=z_scale[:, h, t : t + 1])
+
+        def exponent(h, t):
+            nc.scalar.activation(
+                out=ex[h % 2][:, t, :], in_=th[h % 2][:, t, :], func=ACT.Exp, scale=CAP,
+                bias=neg_max[:, h : h + 1], accum_out=ex_sum[h][:, t : t + 1],
+            )
+
+        def square(h):
+            nc.scalar.activation(out=th[h % 2][:], in_=th[h % 2][:], func=ACT.Square)
+
+        def add_sink(h, c=slice(0, PACK)):
+            nc.vector.tensor_scalar(out=denom[h][:, c], in0=ex_sum[h][:, c], scalar1=sink_exp[:, h : h + 1], scalar2=None, op0=ALU.add)
+
+        def invert(h, c=slice(0, PACK)):
+            nc.vector.reciprocal(out=inv_denom[h][:, c], in_=denom[h][:, c])
+
+        def make_gain(h, c=slice(0, PACK)):
+            nc.vector.tensor_tensor(out=gain[h][:, c], in0=inv_denom[h][:, c], in1=tau32[:, h, c], op=ALU.mult)
+
+        def weigh(h, t):
+            nc.vector.scalar_tensor_tensor(
+                out=grad[:, t, :], in0=pending[("dp", h), t][:], scalar=gain[h][:, t : t + 1], in1=ex[h % 2][:, t, :],
+                op0=ALU.mult, op1=ALU.mult, accum_out=dot[h][:, t : t + 1],
+            )
+
+        def make_shift(h, c):
+            nc.vector.tensor_tensor(out=shift[h][:, c], in0=dot[h][:, c], in1=inv_denom[h][:, c], op=ALU.mult)
+
+        def centre(h, t):
+            nc.vector.scalar_tensor_tensor(
+                out=grad[:, t, :], in0=ex[h % 2][:, t, :], scalar=shift[h][:, t : t + 1], in1=grad[:, t, :],
+                op0=ALU.mult, op1=ALU.subtract,
+            )
+
+        def finish_g(h, part=0, parts=1):
+            n = S // parts
+            cols = slice(part * n, (part + 1) * n)
+            nc.vector.scalar_tensor_tensor(
+                out=stage["gi"][:].rearrange("p (j t) -> p j t", t=PACK)[:, cols, :],
+                in0=th[h % 2][:, :, cols].rearrange("p t j -> p j t"),
+                scalar=1.0,
+                in1=grad[:, :, cols].rearrange("p t j -> p j t"),
+                op0=ALU.subtract, op1=ALU.mult,
+            )
+
+        def gain_result(h, b):
+            nc.vector.scalar_tensor_tensor(
+                out=res[h % 2][:, b, :], in0=pending[("out", h), b][:], scalar=inv_root_d, in1=a_free[:, h, :],
+                op0=ALU.mult, op1=ALU.mult,
+            )
+
+        def round_result(h, b):
+            nc.scalar.copy(out=res16[:, b, :], in_=res[h % 2][:, b, :])
+
+        def store_result(h, blocks):
+            view = out_0[h].rearrange("(b p) d -> p b d", p=P)
+            nc.sync.dma_start(out=view[:, blocks, :], in_=res[h % 2][:, blocks, :])
+
+        words_out = out_1[0].rearrange("p m t -> p (m t)").bitcast(I32)
+
+        def store_words(h, part=0, parts=1):
+            n = W // parts
+            nc.sync.dma_start(
+                out=words_out[:, h * W + part * n : h * W + (part + 1) * n],
+                in_=out_codes[:, h, part * n : (part + 1) * n].bitcast(I32),
+            )
+
+        def store_scales(cols, last):
+            for quad in range(4):
+                (nc.scalar if last and quad % 2 else nc.sync).dma_start(
+                    out=out_2[0, 4 * quad : 4 * quad + 4, cols].bitcast(I32),
+                    in_=out_scales[32 * quad : 32 * quad + 4, cols].bitcast(I32),
+                )
+
+        nc.scalar.dma_start(out=a_part[:], in_=a.rearrange("h (p t) -> p h t", t=PACK))
+        nc.scalar.dma_start(out=sink16[:], in_=sink.partition_broadcast(P))
+        nc.scalar.dma_start(out=tau16[:], in_=tau.rearrange("h (p t) -> p h t", t=PACK))
+        lo, hi = slice(0, 2), slice(2, 4)
+        load("k", k, 0, lo)
+        load("k", k, 0, hi)
+        load("q", q, 0, lo)
+        load("do", d_o, 0, lo)
+        load("q", q, 0, hi)
+        load("do", d_o, 0, hi)
+        load("v", v, 0, lo)
+        load("v", v, 0, hi)
+        for h in range(1, H):
+            load("k", k, h)
+            load("q", q, h)
+            load("do", d_o, h)
+            load("v", v, h)
+            if h == 1:
+                nc.sync.dma_start(out=a_free[:].rearrange("p h d -> p (h d)"), in_=a.rearrange("h d -> (h d)").partition_broadcast(P))
+        make_identity(nc, ident32[:])
+        make_identity(nc, ident16[:])
+
+        nc.vector.tensor_scalar(out=neg_max[:], in0=sink16[:], scalar1=CAP, scalar2=-1.0, op0=ALU.max, op1=ALU.mult)
+        nc.vector.tensor_copy(out=tau32[:], in_=tau16[:])
+        nc.vector.tensor_scalar(out=z_scale[:], in0=tau16[:], scalar1=inv_root_d / CAP, scalar2=None, op0=ALU.mult)
+        nc.vector.tensor_tensor(out=sink_gap[:], in0=sink16[:], in1=neg_max[:], op=ALU.add)
+        nc.scalar.activation(out=sink_exp[:], in_=sink_gap[:], func=ACT.Exp)
+
+        def both(fn, *args):
+            for half in range(2):
+                fn(args[0], *args[1:-1], half, args[-1])
+
+        both(turn_rows, ("kd", 0), rows["k"][0], "vector")
+        turn_rows(("qd", 0), rows["q"][0], 0, "scalar")
+        turn_rows(("dod", 0), rows["do"][0], 0, "vector")
+        turn_rows(("qd", 0), rows["q"][0], 1, "scalar")
+        turn_rows(("dod", 0), rows["do"][0], 1, "vector")
+        for half in range(2):
+            take_gained_keys(0, half)
+            take_turned(("qd", 0), half, "scalar")
+        quantise("kd", 0, 0, 2)
+        quantise("kd", 0, 1, 2)
+        quantise("qd", 0, 0, 2)
+        take_turned(("dod", 0), 0, "vector")
+        take_turned(("dod", 0), 1, "vector")
+        quantise("qd", 0, 1, 2)
+        quantise("dod", 0)
+        for t in range(2):
+            product("z", 0, t, "qd", "kd", "scalar")
+        both(turn_rows, ("vd", 0), rows["v"][0], "vector")
+        for t in range(2, 4):
+            product("z", 0, t, "qd", "kd", "scalar")
+        for t in range(PACK):
+            softcap(0, t)
+            if t % 2 == 1:
+                exponent(0, t - 1)
+                exponent(0, t)
+        both(take_turned, ("vd", 0), "vector")
+        both(turn_rows, ("kd", 1), rows["k"][1], "vector")
+        add_sink(0, lo)
+        quantise("vd", 0)
+        invert(0, lo)
+        take_gained_keys(1, 0)
+        make_gain(0, lo)
+        take_gained_keys(1, 1)
+        for t in range(2):
+            product("dp", 0, t, "dod", "vd", "vector")
+        both(turn_rows, ("qd", 1), rows["q"][1], "scalar")
+        both(take_turned, ("qd", 1), "scalar")
+
+        for h in range(H):
+            nxt = h + 1 < H
+            nxt2 = h + 2 < H
+            if h == 0:
+                for t in range(2, 4):
+                    product("dp", h, t, "dod", "vd", "vector")
+                weigh(h, 0)
+                add_sink(0, hi)
+                weigh(h, 1)
+                invert(0, hi)
+                quantise("kd", 1)
+                make_gain(0, hi)
+                quantise("qd", 1)
+            else:
+                for t in range(2):
+                    product("dp", h, t, "dod", "vd", "vector")
+                add_sink(h)
+                gain_result(h - 1, 2)
+                round_result(h - 1, 2)
+                invert(h)
+                gain_result(h - 1, 3)
+                round_result(h - 1, 3)
+                store_result(h - 1, hi)
+                for t in range(2, 4):
+                    product("dp", h, t, "dod", "vd", "vector")
+                make_gain(h)
+                both(turn_rows, ("od", h - 1), res16, "scalar")
+                both(take_turned, ("od", h - 1), "scalar")
+                if nxt:
+                    quantise("kd", h + 1)
+                weigh(h, 0)
+                if nxt:
+                    quantise("qd", h + 1)
+                weigh(h, 1)
+            square(h)
+            if nxt:
+                for t in range(PACK):
+                    product("z", h + 1, t, "qd", "kd", "scalar")
+                for t in range(PACK):
+                    softcap(h + 1, t)
+            for half in range(2):
+                weave_q(h, half)
+            for half in range(2):
+                take_woven(h, half)
+            weigh(h, 2)
+            make_shift(h, lo)
+            weigh(h, 3)
+            centre(h, 0)
+            make_shift(h, hi)
+            for t in range(1, PACK):
+                centre(h, t)
+            if nxt:
+                for t in range(PACK):
+                    exponent(h + 1, t)
+            if h > 0:
+                quantise("od", h - 1)
+                store_words(h - 1)
+                if h == H - 1:
+                    store_scales(slice(0, (H - 1) * W), False)
+            if nxt2:
+                both(turn_rows, ("kd", h + 2), rows["k"][h + 2], "vector")
+            if nxt:
+                both(turn_rows, ("dod", h + 1), rows["do"][h + 1], "scalar")
+                both(take_turned, ("dod", h + 1), "scalar")
+                both(turn_rows, ("vd", h + 1), rows["v"][h + 1], "scalar")
+                both(take_turned, ("vd", h + 1), "scalar")
+                if nxt2:
+                    both(turn_rows, ("qd", h + 2), rows["q"][h + 2], "scalar")
+                    both(take_turned, ("qd", h + 2), "scalar")
+                finish_g(h, 0, 2)
+                quantise("qi", h)
+                finish_g(h, 1, 2)
+                quantise("gi", h, 0, 2)
+                if nxt2:
+                    take_gained_keys(h + 2, 0)
+                quantise("gi", h, 1, 2)
+                if nxt2:
+                    take_gained_keys(h + 2, 1)
+                for b in range(PACK):
+                    product("out", h, b, "gi", "qi", "vector")
+                quantise("dod", h + 1)
+                gain_result(h, 0)
+                round_result(h, 0)
+                quantise("vd", h + 1)
+                gain_result(h, 1)
+                round_result(h, 1)
+                store_result(h, lo)
+        h = H - 1
+        for step in range(PACK + 4):
+            if 0 <= step - 3 < PACK:
+                turn_block(h, step - 3)
+            if step < PACK:
+                finish_g(h, step, PACK)
+            if step == 0:
+                quantise("qi", h)
+            if 0 <= step - 1 < PACK:
+                quantise("gi", h, step - 1, PACK)
+                product("out", h, step - 1, "gi", "qi", "vector")
+            if 0 <= step - 2 < PACK:
+                gain_result(h, step - 2)
+                round_result(h, step - 2)
+                store_result(h, slice(step - 2, step - 1))
+            if 0 <= step - 4 < PACK:
+                quantise("od", h, step - 4, PACK)
+            if 0 <= step - 3 < PACK:
+                take_block(h, step - 3)
+        store_words(H - 1)
+        store_scales(slice((H - 1) * W, H * W), True)

@@ -20,6 +20,35 @@ ACT = mybir.ActivationFunctionType
 P = 128
 PACK = 4
 W = 512
+BANKS = 8
+LAST = H - 1
+PAIRS = (slice(0, 2), slice(2, 4))
+
+OPENING = """
+    warm:0 warm:0 warm:0 warm:0 warm:0 warm:0 turn_k:0 gain_keys:0 turn_k:0 turn_q:0 warm:0 turn_do:0 turn_q:0
+    hquant_k:0 take_q:0 gain_keys:0 take_do:0 hquant_q:0 turn_do:0 hquant_k:0 logits:0 vtake_q:0 logits:0
+    hquant_q:0 turn_v:0 take_do:0 softcap:0 turn_v:0 softcap:0 logits:0 quant_do:0 vtake_v:0 vtake_v:0 logits:0
+    quant_v:0 exp:0 turn_q:1 turn_k:1 exp:0 add_sink:0 softcap:0 invert:0 turn_k:1 gain:0 vtake_q:1 softcap:0
+    gain_keys:1 dprob:0 gain_keys:1 exp:0 weigh:0 exp:0 turn_q:1
+"""
+STEADY = """
+    softcap:0 add_sink:0 quant_g:-1 take_do:0 turn_v:+1 quant_k:+1 take_do:0 take_q:+1 finish:-1 result:-1
+    take_q:+1 exp:0 result:-1 quant_do:0 turn_k:+2 quant_q:+1 invert:0 quant_g:-1 exp:0 dprob:0 add_sink:0
+    turn_k:+2 scale:-1 dprob:0 gain:0 invert:0 square:0 scale:-1 take_v:+1 gain_keys:+2 round:-1 result:-1
+    round:-1 weave:0 weave:0 weigh:0 gain:0 result:-1 gain_keys:+2 square:0 scale:-1 dprob:0 logits:+1 store:-1
+    dprob:0 turn_v:+1 weigh:0 weave:0 logits:+1 weigh:0 scale:-1 turn_out:-1 shift:0 weigh:0 logits:+1 logits:+1
+    centre:0 round:-1 shift:0 take_v:+1 weave:0 round:-1 centre:0 centre:0 turn_q:+2 centre:0 softcap:+1
+    quant_v:+1 turn_do:+1 finish:0 turn_out:-1 softcap:+1 softcap:+1 take_out:-1 store:-1 take_out:-1 finish:0
+    finish:0 exp:+1 turn_q:+2 turn_do:+1 quant_qi:0 exp:+1 quant_out:-1 store_words:-1
+"""
+CLOSING = """
+    finish:3 finish:3 quant_g_block:3 finish:3 result:3 quant_g_block:3 finish:3 quant_g_block:3 scale:3
+    store_block:3 result:3 quant_g_block:3 scale:3 store_block:3 round:3 result:3 result:3 round:3 scale:3
+    store_block:3 scale16_last:3 round:3 turn_block:3 take_block:3 scale:3 store_block:3 quant_block:3
+    turn_block:3 turn_block:3 take_block:3 turn_block:3 quant_block:3 take_block:3 vtake_block:3 quant_block:3
+    quant_block:3 store_scales:3
+"""
+CLOSING_STEPS = ("finish", "quant_g", "result", "scale", "round", "turn_out", "take_out", "quant_out", "store", "store_words")
 
 
 def tile_softcapsinkattentionbackward_x1_kernel(tc, q, k, v, d_o, sink, tau, a, out_0, out_1, out_2):
@@ -34,104 +63,118 @@ def tile_softcapsinkattentionbackward_x1_kernel(tc, q, k, v, d_o, sink, tau, a, 
             return [sb.tile(shape, dtype, name="%s%d" % (name, n), align_bytes=64) for n in range(count)]
 
         rows = {name: tiles(name, H, [P, PACK, D], BF16) for name in ("q", "k", "v", "do")}
-        names = ("qd", "kd", "dod", "vd", "qi", "gi")
-        stage = {name: sb.tile([P, W * PACK], BF16, name="stage_" + name, align_bytes=64) for name in names + ("od",)}
-        codes = {name: tiles("codes_" + name, 2, [P, W], U32) for name in names}
-        scales = {name: tiles("scales_" + name, 2, [P, W], U8) for name in names}
-        out_codes = sb.tile([P, H, W], U32, align_bytes=64)
+        operands = ("q", "k", "do", "v", "qi", "g")
+        stage = {name: sb.tile([P, W * PACK], BF16, name="stage_" + name, align_bytes=64) for name in operands + ("out",)}
+        codes = {name: tiles("codes_" + name, 2, [P, W], U32) for name in operands}
+        scales = {name: tiles("scales_" + name, 2, [P, W], U8) for name in operands}
+        out_codes = sb.tile([P, H * W], U32, align_bytes=64)
         out_scales = sb.tile([P, H * W], U8, align_bytes=64)
-        th = tiles("th", 2, [P, PACK, S], F32)
+        th = tiles("th", 2, [P, P, PACK, PACK], F32)
         ex = tiles("ex", 2, [P, PACK, S], F32)
-        grad = sb.tile([P, PACK, S], F32, align_bytes=64)
+        grad = sb.tile([P, P, PACK, PACK], F32, align_bytes=64)
         res = tiles("res", 2, [P, PACK, D], F32)
         res16 = sb.tile([P, PACK, D], BF16, align_bytes=64)
-        banks = [ps.tile([P, W], F32, name="bank%d" % n) for n in range(8)]
-        turn = {"vector": [], "scalar": []}
 
-        def next_bank(reader):
-            turn[reader].append(0)
-            first = 0 if reader == "vector" else 4
-            return banks[first + (len(turn[reader]) - 1) % 4]
-
-        a_part = sb.tile([P, H, PACK], BF16)
-        tau16 = sb.tile([P, H, PACK], BF16)
-        sink16 = sb.tile([P, H], BF16)
+        a_first = sb.tile([P, 1, PACK], BF16)
+        a_rest = sb.tile([P, LAST, PACK], BF16)
         a_free = sb.tile([P, H, D], BF16)
+        tau16 = sb.tile([P, H, PACK], BF16)
         tau32 = sb.tile([P, H, PACK], F32)
         z_scale = sb.tile([P, H, PACK], F32)
+        sink16 = sb.tile([P, H], BF16)
         neg_max = sb.tile([P, H], F32)
         sink_gap = sb.tile([P, H], F32)
         sink_exp = sb.tile([P, H], F32)
         ex_sum = tiles("ex_sum", H, [P, PACK], F32)
         denom = tiles("denom", H, [P, PACK], F32)
         inv_denom = tiles("inv_denom", H, [P, PACK], F32)
-        gain = tiles("gain", H, [P, PACK], F32)
-        dot = tiles("dot", H, [P, PACK], F32)
-        shift = tiles("shift", H, [P, PACK], F32)
-        ident32 = sb.tile([P, P], F32)
+        row_gain = tiles("row_gain", H, [P, PACK], F32)
+        grad_sum = tiles("grad_sum", H, [P, PACK], F32)
+        kappa = tiles("kappa", H, [P, PACK], F32)
         ident16 = sb.tile([P, P], BF16)
+        ident32 = sb.tile([P, P], F32)
+        shuffle32 = sb.tile([P, P], F32)
 
-        def load(name, src, h, slots=slice(0, PACK)):
-            pattern = "(p t) d -> p t d" if name in ("q", "do") else "(t p) d -> p t d"
-            view = src[h].rearrange(pattern, t=PACK)
-            nc.sync.dma_start(out=rows[name][h][:, slots, :], in_=view[:, slots, :])
+        bank_queue = [ps.tile([P, W], F32, name="bank%d" % n) for n in range(BANKS)]
+        handed_out = []
+        filled = {}
 
-        pending = {}
+        def next_bank():
+            handed_out.append(bank_queue[len(handed_out)])
+            return handed_out[-1]
 
-        def turn_block(h, b):
-            bank = next_bank("scalar")
-            words = res16[:, b, :].bitcast(F32)
-            for u in range(2):
-                nc.tensor.transpose(bank[:, u * P : (u + 1) * P], words[:, u : 2 * P : 2], ident32[:])
-            pending[("od", h), b] = bank
+        def last_read_of(key):
+            bank_queue.append(filled[key])
+            return filled[key]
 
-        def take_block(h, b):
-            nc.scalar.copy(
-                out=stage["od"][:, b * W : (b + 1) * W].bitcast(F32).rearrange("p (c u) -> p c u", u=2),
-                in_=pending[("od", h), b][:, : 2 * P].rearrange("p (u c) -> p c u", u=2),
-            )
-
-        def turn_rows(key, src, half, reader):
-            bank = next_bank(reader)
-            view = bank[:].rearrange("p (u s r) -> p u s r", u=2, s=2)
-            for s in range(2):
-                words = src[:, 2 * half + s, :].bitcast(F32)
-                for u in range(2):
-                    nc.tensor.transpose(view[:, u, s, :], words[:, u : 2 * P : 2], ident32[:])
-            pending[key, half] = bank
-
-        def half_of(name, half):
-            return stage[name][:, half * 1024 : (half + 1) * 1024]
-
-        def take_turned(key, half, engine):
-            bank = pending[key, half]
-            dst = half_of(key[0], half).bitcast(F32).rearrange("p (c u) -> p c u", u=2)
-            src = bank[:].rearrange("p (u c) -> p c u", u=2)
+        def copy_on(engine, dst, src):
             if engine == "scalar":
                 nc.scalar.copy(out=dst, in_=src)
             else:
                 nc.vector.tensor_copy(out=dst, in_=src)
 
-        def take_gained_keys(h, half):
-            bank = pending[("kd", h), half]
+        def quads(ap):
+            return ap.rearrange("p (m n) -> p m n", n=PACK)
+
+        def load(name, src, h, slots):
+            pattern = "(p s) d -> p s d" if name in ("q", "do") else "(s p) d -> p s d"
+            nc.sync.dma_start(out=rows[name][h][:, slots, :], in_=src[h].rearrange(pattern, s=PACK)[:, slots, :])
+
+        def warm(h, part):
+            bank = next_bank()
+            nc.tensor.matmul(
+                out=bank[:], lhsT=ident16[:], rhs=ident16[:].unsqueeze(1).to_broadcast([P, PACK, P]), start=True, stop=True
+            )
+            bank_queue.append(bank)
+
+        def turn(name, h, slots, part):
+            src = res16 if name == "out" else rows[name][h]
+            order = shuffle32 if name in ("k", "v") else ident32
+            bank = next_bank()
+            view = bank[:, : 2 * P * len(slots)].rearrange("p (u s r) -> p u s r", u=2, r=P)
+            for n, slot in enumerate(slots):
+                words = src[:, slot, :].bitcast(F32)
+                for u in range(2):
+                    nc.tensor.transpose(view[:, u, n, :], words[:, u : 2 * P : 2], order[:])
+            filled[name, h, part] = bank
+
+        def take(name, h, columns, part, engine):
+            dst = stage[name][:, part * columns * PACK : (part + 1) * columns * PACK].bitcast(F32)
+            src = last_read_of((name, h, part))[:, : 2 * columns]
+            copy_on(engine, dst.rearrange("p (c u) -> p c u", u=2), src.rearrange("p (u c) -> p c u", u=2))
+
+        def gain_keys(h, half):
+            gains = a_first[:, 0, :] if h == 0 else a_rest[:, h - 1, :]
+            columns = W // 2
             nc.vector.tensor_tensor(
-                out=half_of("kd", half).rearrange("p (c u e) -> p c u e", u=2, e=2),
-                in0=bank[:].bitcast(BF16).rearrange("p (u c e) -> p c u e", u=2, e=2),
-                in1=a_part[:, h, :].rearrange("p (u e) -> p u e", u=2).unsqueeze(1).to_broadcast([P, 256, 2, 2]),
+                out=stage["k"][:, half * columns * PACK : (half + 1) * columns * PACK].rearrange("p (c u e) -> p c u e", u=2, e=2),
+                in0=last_read_of(("k", h, half))[:].bitcast(BF16).rearrange("p (u c e) -> p c u e", u=2, e=2),
+                in1=gains.rearrange("p (u e) -> p u e", u=2).unsqueeze(1).to_broadcast([P, columns, 2, 2]),
                 op=ALU.mult,
             )
 
-        def quantise(name, h, part=0, parts=1):
-            n = W // parts
-            cols = slice(part * n, (part + 1) * n)
-            if name == "od":
-                c, s = out_codes[:, h, cols], out_scales[:, h * W + part * n : h * W + (part + 1) * n]
-            else:
-                c, s = codes[name][h % 2][:, cols], scales[name][h % 2][:, cols]
-            nc.vector.quantize_mx(out=c.bitcast(FP8X4), scales=s, in_=stage[name][:, PACK * part * n : PACK * (part + 1) * n])
+        def weave(h, part):
+            cols = slice(part * P, (part + 1) * P)
+            nc.gpsimd.tensor_scalar(
+                out=stage["qi"][:].rearrange("p (d t) -> p d t", t=PACK)[:, cols, :],
+                in0=rows["q"][h][:, :, cols].rearrange("p t d -> p d t"),
+                scalar1=1.0, scalar2=0.0, op0=ALU.mult, op1=ALU.add,
+            )
 
-        def product(key, h, block, still, moving, reader):
-            bank = next_bank(reader)
+        def quantise(name, h, part, parts):
+            n = W // parts
+            if name == "out":
+                cols = slice(h * W + part * n, h * W + (part + 1) * n)
+                dst, dst_scales = out_codes[:, cols], out_scales[:, cols]
+            else:
+                cols = slice(part * n, (part + 1) * n)
+                dst, dst_scales = codes[name][h % 2][:, cols], scales[name][h % 2][:, cols]
+            nc.vector.quantize_mx(
+                out=dst.bitcast(FP8X4), scales=dst_scales, in_=stage[name][:, PACK * part * n : PACK * (part + 1) * n]
+            )
+
+        def product(name, h, block, still, moving):
+            bank = next_bank()
             cols = slice(block * P, (block + 1) * P)
             nc.tensor.matmul_mx(
                 out=bank[:],
@@ -142,276 +185,188 @@ def tile_softcapsinkattentionbackward_x1_kernel(tc, q, k, v, d_o, sink, tau, a, 
                 start=True,
                 stop=True,
             )
-            pending[(key, h), block] = bank
-
-        def weave_q(h, half):
-            bank = next_bank("scalar")
-            wide = bank[:].bitcast(BF16)
-            for c in range(2):
-                d0 = (2 * half + c) * P
-                nc.tensor.matmul(
-                    out=wide[:, c * W : (c + 1) * W],
-                    lhsT=ident16[:],
-                    rhs=rows["q"][h][:, :, d0 : d0 + P].rearrange("p t d -> p d t"),
-                    start=True,
-                    stop=True,
-                )
-            pending[("qi", h), half] = bank
-
-        def take_woven(h, half):
-            nc.scalar.copy(out=half_of("qi", half), in_=pending[("qi", h), half][:].bitcast(BF16))
+            filled[name, h, block] = bank
 
         def softcap(h, t):
-            nc.scalar.activation(out=th[h % 2][:, t, :], in_=pending[("z", h), t][:], func=ACT.Tanh, scale=z_scale[:, h, t : t + 1])
+            nc.scalar.activation(
+                out=th[h % 2][:, :, t, :], in_=quads(last_read_of(("z", h, t))[:]), func=ACT.Tanh,
+                scale=z_scale[:, h, t : t + 1],
+            )
 
         def exponent(h, t):
             nc.scalar.activation(
-                out=ex[h % 2][:, t, :], in_=th[h % 2][:, t, :], func=ACT.Exp, scale=CAP,
+                out=quads(ex[h % 2][:, t, :]), in_=th[h % 2][:, :, t, :], func=ACT.Exp, scale=CAP,
                 bias=neg_max[:, h : h + 1], accum_out=ex_sum[h][:, t : t + 1],
             )
 
-        def square(h):
-            nc.scalar.activation(out=th[h % 2][:], in_=th[h % 2][:], func=ACT.Square)
+        def square(h, half):
+            part = th[h % 2][:, :, PAIRS[half], :]
+            nc.scalar.activation(out=part, in_=part, func=ACT.Square)
 
-        def add_sink(h, c=slice(0, PACK)):
-            nc.vector.tensor_scalar(out=denom[h][:, c], in0=ex_sum[h][:, c], scalar1=sink_exp[:, h : h + 1], scalar2=None, op0=ALU.add)
+        def add_sink(h, half):
+            ts = PAIRS[half]
+            nc.scalar.activation(out=denom[h][:, ts], in_=ex_sum[h][:, ts], func=ACT.Identity, bias=sink_exp[:, h : h + 1])
 
-        def invert(h, c=slice(0, PACK)):
-            nc.vector.reciprocal(out=inv_denom[h][:, c], in_=denom[h][:, c])
+        def invert(h, half):
+            nc.vector.reciprocal(out=inv_denom[h][:, PAIRS[half]], in_=denom[h][:, PAIRS[half]])
 
-        def make_gain(h, c=slice(0, PACK)):
-            nc.vector.tensor_tensor(out=gain[h][:, c], in0=inv_denom[h][:, c], in1=tau32[:, h, c], op=ALU.mult)
+        def gain(h, half):
+            ts = PAIRS[half]
+            nc.gpsimd.tensor_tensor(out=row_gain[h][:, ts], in0=inv_denom[h][:, ts], in1=tau32[:, h, ts], op=ALU.mult)
 
         def weigh(h, t):
             nc.vector.scalar_tensor_tensor(
-                out=grad[:, t, :], in0=pending[("dp", h), t][:], scalar=gain[h][:, t : t + 1], in1=ex[h % 2][:, t, :],
-                op0=ALU.mult, op1=ALU.mult, accum_out=dot[h][:, t : t + 1],
+                out=grad[:, :, t, :], in0=quads(last_read_of(("dp", h, t))[:]), scalar=row_gain[h][:, t : t + 1],
+                in1=quads(ex[h % 2][:, t, :]), op0=ALU.mult, op1=ALU.mult, accum_out=grad_sum[h][:, t : t + 1],
             )
 
-        def make_shift(h, c):
-            nc.vector.tensor_tensor(out=shift[h][:, c], in0=dot[h][:, c], in1=inv_denom[h][:, c], op=ALU.mult)
+        def shift(h, half):
+            ts = PAIRS[half]
+            nc.vector.tensor_tensor(out=kappa[h][:, ts], in0=grad_sum[h][:, ts], in1=inv_denom[h][:, ts], op=ALU.mult)
 
         def centre(h, t):
             nc.vector.scalar_tensor_tensor(
-                out=grad[:, t, :], in0=ex[h % 2][:, t, :], scalar=shift[h][:, t : t + 1], in1=grad[:, t, :],
+                out=grad[:, :, t, :], in0=quads(ex[h % 2][:, t, :]), scalar=kappa[h][:, t : t + 1], in1=grad[:, :, t, :],
                 op0=ALU.mult, op1=ALU.subtract,
             )
 
-        def finish_g(h, part=0, parts=1):
-            n = S // parts
-            cols = slice(part * n, (part + 1) * n)
+        def finish(h, b):
+            ms = slice(32 * b, 32 * (b + 1))
             nc.vector.scalar_tensor_tensor(
-                out=stage["gi"][:].rearrange("p (j t) -> p j t", t=PACK)[:, cols, :],
-                in0=th[h % 2][:, :, cols].rearrange("p t j -> p j t"),
+                out=stage["g"][:, b * P * PACK : (b + 1) * P * PACK].rearrange("p (n ct) -> p ct n", n=PACK),
+                in0=th[h % 2][:, ms, :, :].rearrange("p c t n -> p (c t) n"),
                 scalar=1.0,
-                in1=grad[:, :, cols].rearrange("p t j -> p j t"),
+                in1=grad[:, ms, :, :].rearrange("p c t n -> p (c t) n"),
                 op0=ALU.subtract, op1=ALU.mult,
             )
 
-        def gain_result(h, b):
+        def scale_into(dst, bank, h):
             nc.vector.scalar_tensor_tensor(
-                out=res[h % 2][:, b, :], in0=pending[("out", h), b][:], scalar=inv_root_d, in1=a_free[:, h, :],
-                op0=ALU.mult, op1=ALU.mult,
+                out=dst, in0=bank[:], scalar=inv_root_d, in1=a_free[:, h, :], op0=ALU.mult, op1=ALU.mult
             )
 
-        def round_result(h, b):
-            nc.scalar.copy(out=res16[:, b, :], in_=res[h % 2][:, b, :])
-
-        def store_result(h, blocks):
+        def store(h, blocks):
             view = out_0[h].rearrange("(b p) d -> p b d", p=P)
             nc.sync.dma_start(out=view[:, blocks, :], in_=res[h % 2][:, blocks, :])
 
-        words_out = out_1[0].rearrange("p m t -> p (m t)").bitcast(I32)
+        def store_words(cols):
+            words_out = out_1[0].rearrange("p m t -> p (m t)").bitcast(I32)
+            nc.sync.dma_start(out=words_out[:, cols], in_=out_codes[:, cols].bitcast(I32))
 
-        def store_words(h, part=0, parts=1):
-            n = W // parts
-            nc.sync.dma_start(
-                out=words_out[:, h * W + part * n : h * W + (part + 1) * n],
-                in_=out_codes[:, h, part * n : (part + 1) * n].bitcast(I32),
-            )
-
-        def store_scales(cols, last):
-            for quad in range(4):
-                (nc.scalar if last and quad % 2 else nc.sync).dma_start(
-                    out=out_2[0, 4 * quad : 4 * quad + 4, cols].bitcast(I32),
-                    in_=out_scales[32 * quad : 32 * quad + 4, cols].bitcast(I32),
+        def store_scales(cols, queues):
+            for quadrant in range(4):
+                queues[quadrant % len(queues)].dma_start(
+                    out=out_2[0, 4 * quadrant : 4 * quadrant + 4, cols].bitcast(I32),
+                    in_=out_scales[32 * quadrant : 32 * quadrant + 4, cols].bitcast(I32),
                 )
 
-        nc.scalar.dma_start(out=a_part[:], in_=a.rearrange("h (p t) -> p h t", t=PACK))
-        nc.scalar.dma_start(out=sink16[:], in_=sink.partition_broadcast(P))
-        nc.scalar.dma_start(out=tau16[:], in_=tau.rearrange("h (p t) -> p h t", t=PACK))
-        lo, hi = slice(0, 2), slice(2, 4)
-        load("k", k, 0, lo)
-        load("k", k, 0, hi)
-        load("q", q, 0, lo)
-        load("do", d_o, 0, lo)
-        load("q", q, 0, hi)
-        load("do", d_o, 0, hi)
-        load("v", v, 0, lo)
-        load("v", v, 0, hi)
-        for h in range(1, H):
-            load("k", k, h)
-            load("q", q, h)
-            load("do", d_o, h)
-            load("v", v, h)
-            if h == 1:
-                nc.sync.dma_start(out=a_free[:].rearrange("p h d -> p (h d)"), in_=a.rearrange("h d -> (h d)").partition_broadcast(P))
-        make_identity(nc, ident32[:])
-        make_identity(nc, ident16[:])
+        def store_head_words(h, part):
+            store_words(slice(h * W, (h + 1) * W))
+            if h == LAST - 1:
+                store_scales(slice(0, LAST * W), [nc.sync])
 
-        nc.vector.tensor_scalar(out=neg_max[:], in0=sink16[:], scalar1=CAP, scalar2=-1.0, op0=ALU.max, op1=ALU.mult)
-        nc.vector.tensor_copy(out=tau32[:], in_=tau16[:])
-        nc.vector.tensor_scalar(out=z_scale[:], in0=tau16[:], scalar1=inv_root_d / CAP, scalar2=None, op0=ALU.mult)
-        nc.vector.tensor_tensor(out=sink_gap[:], in0=sink16[:], in1=neg_max[:], op=ALU.add)
+        def quantise_block(h, b):
+            quantise("out", h, b, PACK)
+            store_words(slice(h * W + b * P, h * W + (b + 1) * P))
+
+        steps = {
+            "warm": warm,
+            "gain_keys": gain_keys,
+            "weave": weave,
+            "logits": lambda h, t: product("z", h, t, "q", "k"),
+            "softcap": softcap,
+            "exp": exponent,
+            "square": square,
+            "add_sink": add_sink,
+            "invert": invert,
+            "gain": gain,
+            "dprob": lambda h, t: product("dp", h, t, "do", "v"),
+            "weigh": weigh,
+            "shift": shift,
+            "centre": centre,
+            "finish": finish,
+            "quant_g": lambda h, half: quantise("g", h, half, 2),
+            "result": lambda h, b: product("gq", h, b, "g", "qi"),
+            "scale": lambda h, b: scale_into(res[h % 2][:, b, :], last_read_of(("gq", h, b)), h),
+            "round": lambda h, b: nc.scalar.copy(out=res16[:, b, :], in_=res[h % 2][:, b, :]),
+            "store": lambda h, half: store(h, PAIRS[half]),
+            "store_words": store_head_words,
+            "quant_g_block": lambda h, b: quantise("g", h, b, PACK),
+            "scale16_last": lambda h, part: scale_into(res16[:, PACK - 1, :], filled["gq", h, PACK - 1], h),
+            "store_block": lambda h, b: store(h, slice(b, b + 1)),
+            "turn_block": lambda h, b: turn("out", h, [b], b),
+            "take_block": lambda h, b: take("out", h, P, b, "scalar"),
+            "vtake_block": lambda h, b: take("out", h, P, b, "vector"),
+            "quant_block": quantise_block,
+            "store_scales": lambda h, part: store_scales(slice(h * W, (h + 1) * W), [nc.sync, nc.scalar]),
+        }
+
+        def operand_steps(name):
+            return {
+                "turn_" + name: lambda h, half: turn(name, h, [2 * half, 2 * half + 1], half),
+                "take_" + name: lambda h, half: take(name, h, W // 2, half, "scalar"),
+                "vtake_" + name: lambda h, half: take(name, h, W // 2, half, "vector"),
+                "quant_" + name: lambda h, part: quantise(name, h, 0, 1),
+                "hquant_" + name: lambda h, half: quantise(name, h, half, 2),
+            }
+
+        tables = [steps] + [operand_steps(name) for name in ("q", "k", "do", "v", "qi", "out")]
+        parts_done = {}
+
+        def run(name, h):
+            family = name.replace("vtake", "take").replace("hquant", "quant")
+            part = parts_done.get((family, h), 0)
+            parts_done[family, h] = part + 1
+            [table for table in tables if name in table][0][name](h, part)
+
+        def tokens(text):
+            return [(token.split(":")[0], int(token.split(":")[1])) for token in text.split()]
+
+        a_view = a.rearrange("h (p t) -> p h t", t=PACK)
+        nc.scalar.dma_start(out=a_first[:], in_=a_view[:, 0:1, :])
+        nc.scalar.dma_start(out=sink16[:], in_=sink.partition_broadcast(P))
+        load("k", k, 0, PAIRS[0])
+        load("k", k, 0, PAIRS[1])
+        load("q", q, 0, PAIRS[0])
+        nc.sync.dma_start(out=tau16[:], in_=tau.rearrange("h (p t) -> p h t", t=PACK))
+        load("do", d_o, 0, PAIRS[0])
+        load("q", q, 0, PAIRS[1])
+        load("do", d_o, 0, PAIRS[1])
+        load("v", v, 0, PAIRS[0])
+        load("v", v, 0, PAIRS[1])
+        nc.sync.dma_start(out=a_rest[:], in_=a_view[:, 1:H, :])
+        for h in range(1, H):
+            if h == LAST:
+                nc.sync.dma_start(
+                    out=a_free[:].rearrange("p h d -> p (h d)"), in_=a.rearrange("h d -> (h d)").partition_broadcast(P)
+                )
+            for name, src in (("k", k), ("q", q), ("do", d_o), ("v", v)):
+                load(name, src, h, slice(0, PACK))
+
+        make_identity(nc, ident16[:])
+        make_identity(nc, ident32[:])
+        nc.gpsimd.tensor_copy(
+            out=shuffle32[:].rearrange("p (c n) -> p c n", n=PACK), in_=ident32[:].rearrange("p (n c) -> p c n", n=PACK)
+        )
+        nc.gpsimd.tensor_scalar(out=neg_max[:], in0=sink16[:], scalar1=CAP, scalar2=-1.0, op0=ALU.max, op1=ALU.mult)
+        nc.gpsimd.tensor_tensor(out=sink_gap[:], in0=sink16[:], in1=neg_max[:], op=ALU.add)
+        nc.gpsimd.tensor_scalar(
+            out=z_scale[:], in0=tau16[:], scalar1=inv_root_d / CAP, scalar2=0.0, op0=ALU.mult, op1=ALU.add
+        )
+        nc.gpsimd.tensor_copy(out=tau32[:], in_=tau16[:])
         nc.scalar.activation(out=sink_exp[:], in_=sink_gap[:], func=ACT.Exp)
 
-        def both(fn, *args):
-            for half in range(2):
-                fn(args[0], *args[1:-1], half, args[-1])
-
-        both(turn_rows, ("kd", 0), rows["k"][0], "vector")
-        turn_rows(("qd", 0), rows["q"][0], 0, "scalar")
-        turn_rows(("dod", 0), rows["do"][0], 0, "vector")
-        turn_rows(("qd", 0), rows["q"][0], 1, "scalar")
-        turn_rows(("dod", 0), rows["do"][0], 1, "vector")
-        for half in range(2):
-            take_gained_keys(0, half)
-            take_turned(("qd", 0), half, "scalar")
-        quantise("kd", 0, 0, 2)
-        quantise("kd", 0, 1, 2)
-        quantise("qd", 0, 0, 2)
-        take_turned(("dod", 0), 0, "vector")
-        take_turned(("dod", 0), 1, "vector")
-        quantise("qd", 0, 1, 2)
-        quantise("dod", 0)
-        for t in range(2):
-            product("z", 0, t, "qd", "kd", "scalar")
-        both(turn_rows, ("vd", 0), rows["v"][0], "vector")
-        for t in range(2, 4):
-            product("z", 0, t, "qd", "kd", "scalar")
-        for t in range(PACK):
-            softcap(0, t)
-            if t % 2 == 1:
-                exponent(0, t - 1)
-                exponent(0, t)
-        both(take_turned, ("vd", 0), "vector")
-        both(turn_rows, ("kd", 1), rows["k"][1], "vector")
-        add_sink(0, lo)
-        quantise("vd", 0)
-        invert(0, lo)
-        take_gained_keys(1, 0)
-        make_gain(0, lo)
-        take_gained_keys(1, 1)
-        for t in range(2):
-            product("dp", 0, t, "dod", "vd", "vector")
-        both(turn_rows, ("qd", 1), rows["q"][1], "scalar")
-        both(take_turned, ("qd", 1), "scalar")
-
-        for h in range(H):
-            nxt = h + 1 < H
-            nxt2 = h + 2 < H
-            if h == 0:
-                for t in range(2, 4):
-                    product("dp", h, t, "dod", "vd", "vector")
-                weigh(h, 0)
-                add_sink(0, hi)
-                weigh(h, 1)
-                invert(0, hi)
-                quantise("kd", 1)
-                make_gain(0, hi)
-                quantise("qd", 1)
-            else:
-                for t in range(2):
-                    product("dp", h, t, "dod", "vd", "vector")
-                add_sink(h)
-                gain_result(h - 1, 2)
-                round_result(h - 1, 2)
-                invert(h)
-                gain_result(h - 1, 3)
-                round_result(h - 1, 3)
-                store_result(h - 1, hi)
-                for t in range(2, 4):
-                    product("dp", h, t, "dod", "vd", "vector")
-                make_gain(h)
-                both(turn_rows, ("od", h - 1), res16, "scalar")
-                both(take_turned, ("od", h - 1), "scalar")
-                if nxt:
-                    quantise("kd", h + 1)
-                weigh(h, 0)
-                if nxt:
-                    quantise("qd", h + 1)
-                weigh(h, 1)
-            square(h)
-            if nxt:
-                for t in range(PACK):
-                    product("z", h + 1, t, "qd", "kd", "scalar")
-                for t in range(PACK):
-                    softcap(h + 1, t)
-            for half in range(2):
-                weave_q(h, half)
-            for half in range(2):
-                take_woven(h, half)
-            weigh(h, 2)
-            make_shift(h, lo)
-            weigh(h, 3)
-            centre(h, 0)
-            make_shift(h, hi)
-            for t in range(1, PACK):
-                centre(h, t)
-            if nxt:
-                for t in range(PACK):
-                    exponent(h + 1, t)
-            if h > 0:
-                quantise("od", h - 1)
-                store_words(h - 1)
-                if h == H - 1:
-                    store_scales(slice(0, (H - 1) * W), False)
-            if nxt2:
-                both(turn_rows, ("kd", h + 2), rows["k"][h + 2], "vector")
-            if nxt:
-                both(turn_rows, ("dod", h + 1), rows["do"][h + 1], "scalar")
-                both(take_turned, ("dod", h + 1), "scalar")
-                both(turn_rows, ("vd", h + 1), rows["v"][h + 1], "scalar")
-                both(take_turned, ("vd", h + 1), "scalar")
-                if nxt2:
-                    both(turn_rows, ("qd", h + 2), rows["q"][h + 2], "scalar")
-                    both(take_turned, ("qd", h + 2), "scalar")
-                finish_g(h, 0, 2)
-                quantise("qi", h)
-                finish_g(h, 1, 2)
-                quantise("gi", h, 0, 2)
-                if nxt2:
-                    take_gained_keys(h + 2, 0)
-                quantise("gi", h, 1, 2)
-                if nxt2:
-                    take_gained_keys(h + 2, 1)
-                for b in range(PACK):
-                    product("out", h, b, "gi", "qi", "vector")
-                quantise("dod", h + 1)
-                gain_result(h, 0)
-                round_result(h, 0)
-                quantise("vd", h + 1)
-                gain_result(h, 1)
-                round_result(h, 1)
-                store_result(h, lo)
-        h = H - 1
-        for step in range(PACK + 4):
-            if 0 <= step - 3 < PACK:
-                turn_block(h, step - 3)
-            if step < PACK:
-                finish_g(h, step, PACK)
-            if step == 0:
-                quantise("qi", h)
-            if 0 <= step - 1 < PACK:
-                quantise("gi", h, step - 1, PACK)
-                product("out", h, step - 1, "gi", "qi", "vector")
-            if 0 <= step - 2 < PACK:
-                gain_result(h, step - 2)
-                round_result(h, step - 2)
-                store_result(h, slice(step - 2, step - 1))
-            if 0 <= step - 4 < PACK:
-                quantise("od", h, step - 4, PACK)
-            if 0 <= step - 3 < PACK:
-                take_block(h, step - 3)
-        store_words(H - 1)
-        store_scales(slice((H - 1) * W, H * W), True)
+        for name, h in tokens(OPENING):
+            run(name, h)
+        done_early = dict(parts_done)
+        for period in range(H + 1):
+            for name, ahead in tokens(STEADY):
+                h = period + ahead
+                if h < 0 or h > LAST or (h == LAST and name in CLOSING_STEPS):
+                    continue
+                if name != "warm" and done_early.get((name, h), 0) > 0:
+                    done_early[name, h] = done_early[name, h] - 1
+                    continue
+                run(name, h)
+        for name, h in tokens(CLOSING):
+            run(name, h)

import math
from contextlib import ExitStack

import concourse.mybir as mybir
from concourse.masks import make_identity

H, S, D = 4, 512, 512
CAP = 6.0
FLOPS = 3 * 2 * H * S * S * D

F32 = mybir.dt.float32
BF16 = mybir.dt.bfloat16
I32 = mybir.dt.int32
U32 = mybir.dt.uint32
U8 = mybir.dt.uint8
FP8X4 = mybir.dt.float8_e4m3fn_x4
ALU = mybir.AluOpType
ACT = mybir.ActivationFunctionType

P = 128
PACK = 4
W = 512
BANKS = 8
LAST = H - 1
PAIRS = (slice(0, 2), slice(2, 4))

OPENING = """
    warm:0 warm:0 warm:0 warm:0 warm:0 warm:0 turn_k:0 gain_keys:0 turn_k:0 turn_q:0 warm:0 turn_do:0 turn_q:0
    hquant_k:0 take_q:0 gain_keys:0 take_do:0 hquant_q:0 turn_do:0 hquant_k:0 logits:0 vtake_q:0 logits:0
    hquant_q:0 turn_v:0 take_do:0 softcap:0 turn_v:0 softcap:0 logits:0 quant_do:0 vtake_v:0 vtake_v:0 logits:0
    quant_v:0 exp:0 turn_q:1 turn_k:1 exp:0 add_sink:0 softcap:0 invert:0 turn_k:1 gain:0 vtake_q:1 softcap:0
    gain_keys:1 dprob:0 gain_keys:1 exp:0 weigh:0 exp:0 turn_q:1
"""
STEADY = """
    softcap:0 add_sink:0 quant_g:-1 take_do:0 turn_v:+1 quant_k:+1 take_do:0 take_q:+1 finish:-1 result:-1
    take_q:+1 exp:0 result:-1 quant_do:0 turn_k:+2 quant_q:+1 invert:0 quant_g:-1 exp:0 dprob:0 add_sink:0
    turn_k:+2 scale:-1 dprob:0 gain:0 invert:0 square:0 scale:-1 take_v:+1 gain_keys:+2 round:-1 result:-1
    round:-1 weave:0 weave:0 weigh:0 gain:0 result:-1 gain_keys:+2 square:0 scale:-1 dprob:0 logits:+1 store:-1
    dprob:0 turn_v:+1 weigh:0 weave:0 logits:+1 weigh:0 scale:-1 turn_out:-1 shift:0 weigh:0 logits:+1 logits:+1
    centre:0 round:-1 shift:0 take_v:+1 weave:0 round:-1 centre:0 centre:0 turn_q:+2 centre:0 softcap:+1
    quant_v:+1 turn_do:+1 finish:0 turn_out:-1 softcap:+1 softcap:+1 take_out:-1 store:-1 take_out:-1 finish:0
    finish:0 exp:+1 turn_q:+2 turn_do:+1 quant_qi:0 exp:+1 quant_out:-1 store_words:-1
"""
CLOSING = """
    finish:3 finish:3 quant_g_block:3 finish:3 result:3 quant_g_block:3 finish:3 quant_g_block:3 scale:3
    store_block:3 result:3 quant_g_block:3 scale:3 store_block:3 round:3 result:3 result:3 round:3 scale:3
    store_block:3 scale16_last:3 round:3 turn_block:3 take_block:3 scale:3 store_block:3 quant_block:3
    turn_block:3 turn_block:3 take_block:3 turn_block:3 quant_block:3 take_block:3 vtake_block:3 quant_block:3
    quant_block:3 store_scales:3
"""
CLOSING_STEPS = ("finish", "quant_g", "result", "scale", "round", "turn_out", "take_out", "quant_out", "store", "store_words")


def tile_softcapsinkattentionbackward_x1_kernel(tc, q, k, v, d_o, sink, tau, a, out_0, out_1, out_2):
    nc = tc.nc
    inv_root_d = 1.0 / math.sqrt(D)
    with ExitStack() as ctx:
        sb = ctx.enter_context(tc.tile_pool(name="sb", bufs=1))
        ps = ctx.enter_context(tc.psum_pool(name="ps", bufs=1))
        ctx.enter_context(tc.manual_schedule())

        def tiles(name, count, shape, dtype):
            return [sb.tile(shape, dtype, name="%s%d" % (name, n), align_bytes=64) for n in range(count)]

        rows = {name: tiles(name, H, [P, PACK, D], BF16) for name in ("q", "k", "v", "do")}
        operands = ("q", "k", "do", "v", "qi", "g")
        stage = {name: sb.tile([P, W * PACK], BF16, name="stage_" + name, align_bytes=64) for name in operands + ("out",)}
        codes = {name: tiles("codes_" + name, 2, [P, W], U32) for name in operands}
        scales = {name: tiles("scales_" + name, 2, [P, W], U8) for name in operands}
        out_codes = sb.tile([P, H * W], U32, align_bytes=64)
        out_scales = sb.tile([P, H * W], U8, align_bytes=64)
        th = tiles("th", 2, [P, P, PACK, PACK], F32)
        ex = tiles("ex", 2, [P, PACK, S], F32)
        grad = sb.tile([P, P, PACK, PACK], F32, align_bytes=64)
        res = tiles("res", 2, [P, PACK, D], F32)
        res16 = sb.tile([P, PACK, D], BF16, align_bytes=64)

        a_first = sb.tile([P, 1, PACK], BF16)
        a_rest = sb.tile([P, LAST, PACK], BF16)
        a_free = sb.tile([P, H, D], BF16)
        tau16 = sb.tile([P, H, PACK], BF16)
        tau32 = sb.tile([P, H, PACK], F32)
        z_scale = sb.tile([P, H, PACK], F32)
        sink16 = sb.tile([P, H], BF16)
        neg_max = sb.tile([P, H], F32)
        sink_gap = sb.tile([P, H], F32)
        sink_exp = sb.tile([P, H], F32)
        ex_sum = tiles("ex_sum", H, [P, PACK], F32)
        denom = tiles("denom", H, [P, PACK], F32)
        inv_denom = tiles("inv_denom", H, [P, PACK], F32)
        row_gain = tiles("row_gain", H, [P, PACK], F32)
        grad_sum = tiles("grad_sum", H, [P, PACK], F32)
        kappa = tiles("kappa", H, [P, PACK], F32)
        ident16 = sb.tile([P, P], BF16)
        ident32 = sb.tile([P, P], F32)
        shuffle32 = sb.tile([P, P], F32)

        bank_queue = [ps.tile([P, W], F32, name="bank%d" % n) for n in range(BANKS)]
        handed_out = []
        filled = {}

        def next_bank():
            handed_out.append(bank_queue[len(handed_out)])
            return handed_out[-1]

        def last_read_of(key):
            bank_queue.append(filled[key])
            return filled[key]

        def copy_on(engine, dst, src):
            if engine == "scalar":
                nc.scalar.copy(out=dst, in_=src)
            else:
                nc.vector.tensor_copy(out=dst, in_=src)

        def quads(ap):
            return ap.rearrange("p (m n) -> p m n", n=PACK)

        def load(name, src, h, slots):
            pattern = "(p s) d -> p s d" if name in ("q", "do") else "(s p) d -> p s d"
            nc.sync.dma_start(out=rows[name][h][:, slots, :], in_=src[h].rearrange(pattern, s=PACK)[:, slots, :])

        def warm(h, part):
            bank = next_bank()
            nc.tensor.matmul(
                out=bank[:], lhsT=ident16[:], rhs=ident16[:].unsqueeze(1).to_broadcast([P, PACK, P]), start=True, stop=True
            )
            bank_queue.append(bank)

        def turn(name, h, slots, part):
            src = res16 if name == "out" else rows[name][h]
            order = shuffle32 if name in ("k", "v") else ident32
            bank = next_bank()
            view = bank[:, : 2 * P * len(slots)].rearrange("p (u s r) -> p u s r", u=2, r=P)
            for n, slot in enumerate(slots):
                words = src[:, slot, :].bitcast(F32)
                for u in range(2):
                    nc.tensor.transpose(view[:, u, n, :], words[:, u : 2 * P : 2], order[:])
            filled[name, h, part] = bank

        def take(name, h, columns, part, engine):
            dst = stage[name][:, part * columns * PACK : (part + 1) * columns * PACK].bitcast(F32)
            src = last_read_of((name, h, part))[:, : 2 * columns]
            copy_on(engine, dst.rearrange("p (c u) -> p c u", u=2), src.rearrange("p (u c) -> p c u", u=2))

        def gain_keys(h, half):
            gains = a_first[:, 0, :] if h == 0 else a_rest[:, h - 1, :]
            columns = W // 2
            nc.vector.tensor_tensor(
                out=stage["k"][:, half * columns * PACK : (half + 1) * columns * PACK].rearrange("p (c u e) -> p c u e", u=2, e=2),
                in0=last_read_of(("k", h, half))[:].bitcast(BF16).rearrange("p (u c e) -> p c u e", u=2, e=2),
                in1=gains.rearrange("p (u e) -> p u e", u=2).unsqueeze(1).to_broadcast([P, columns, 2, 2]),
                op=ALU.mult,
            )

        def weave(h, part):
            cols = slice(part * P, (part + 1) * P)
            nc.gpsimd.tensor_scalar(
                out=stage["qi"][:].rearrange("p (d t) -> p d t", t=PACK)[:, cols, :],
                in0=rows["q"][h][:, :, cols].rearrange("p t d -> p d t"),
                scalar1=1.0, scalar2=0.0, op0=ALU.mult, op1=ALU.add,
            )

        def quantise(name, h, part, parts):
            n = W // parts
            if name == "out":
                cols = slice(h * W + part * n, h * W + (part + 1) * n)
                dst, dst_scales = out_codes[:, cols], out_scales[:, cols]
            else:
                cols = slice(part * n, (part + 1) * n)
                dst, dst_scales = codes[name][h % 2][:, cols], scales[name][h % 2][:, cols]
            nc.vector.quantize_mx(
                out=dst.bitcast(FP8X4), scales=dst_scales, in_=stage[name][:, PACK * part * n : PACK * (part + 1) * n]
            )

        def product(name, h, block, still, moving):
            bank = next_bank()
            cols = slice(block * P, (block + 1) * P)
            nc.tensor.matmul_mx(
                out=bank[:],
                lhsT=codes[still][h % 2][:, cols].bitcast(FP8X4),
                lhsT_scale=scales[still][h % 2][:, cols],
                rhs=codes[moving][h % 2][:].bitcast(FP8X4),
                rhs_scale=scales[moving][h % 2][:],
                start=True,
                stop=True,
            )
            filled[name, h, block] = bank

        def softcap(h, t):
            nc.scalar.activation(
                out=th[h % 2][:, :, t, :], in_=quads(last_read_of(("z", h, t))[:]), func=ACT.Tanh,
                scale=z_scale[:, h, t : t + 1],
            )

        def exponent(h, t):
            nc.scalar.activation(
                out=quads(ex[h % 2][:, t, :]), in_=th[h % 2][:, :, t, :], func=ACT.Exp, scale=CAP,
                bias=neg_max[:, h : h + 1], accum_out=ex_sum[h][:, t : t + 1],
            )

        def square(h, half):
            part = th[h % 2][:, :, PAIRS[half], :]
            nc.scalar.activation(out=part, in_=part, func=ACT.Square)

        def add_sink(h, half):
            ts = PAIRS[half]
            nc.scalar.activation(out=denom[h][:, ts], in_=ex_sum[h][:, ts], func=ACT.Identity, bias=sink_exp[:, h : h + 1])

        def invert(h, half):
            nc.vector.reciprocal(out=inv_denom[h][:, PAIRS[half]], in_=denom[h][:, PAIRS[half]])

        def gain(h, half):
            ts = PAIRS[half]
            nc.gpsimd.tensor_tensor(out=row_gain[h][:, ts], in0=inv_denom[h][:, ts], in1=tau32[:, h, ts], op=ALU.mult)

        def weigh(h, t):
            nc.vector.scalar_tensor_tensor(
                out=grad[:, :, t, :], in0=quads(last_read_of(("dp", h, t))[:]), scalar=row_gain[h][:, t : t + 1],
                in1=quads(ex[h % 2][:, t, :]), op0=ALU.mult, op1=ALU.mult, accum_out=grad_sum[h][:, t : t + 1],
            )

        def shift(h, half):
            ts = PAIRS[half]
            nc.vector.tensor_tensor(out=kappa[h][:, ts], in0=grad_sum[h][:, ts], in1=inv_denom[h][:, ts], op=ALU.mult)

        def centre(h, t):
            nc.vector.scalar_tensor_tensor(
                out=grad[:, :, t, :], in0=quads(ex[h % 2][:, t, :]), scalar=kappa[h][:, t : t + 1], in1=grad[:, :, t, :],
                op0=ALU.mult, op1=ALU.subtract,
            )

        def finish(h, b):
            ms = slice(32 * b, 32 * (b + 1))
            nc.vector.scalar_tensor_tensor(
                out=stage["g"][:, b * P * PACK : (b + 1) * P * PACK].rearrange("p (n ct) -> p ct n", n=PACK),
                in0=th[h % 2][:, ms, :, :].rearrange("p c t n -> p (c t) n"),
                scalar=1.0,
                in1=grad[:, ms, :, :].rearrange("p c t n -> p (c t) n"),
                op0=ALU.subtract, op1=ALU.mult,
            )

        def scale_into(dst, bank, h):
            nc.vector.scalar_tensor_tensor(
                out=dst, in0=bank[:], scalar=inv_root_d, in1=a_free[:, h, :], op0=ALU.mult, op1=ALU.mult
            )

        def store(h, blocks):
            view = out_0[h].rearrange("(b p) d -> p b d", p=P)
            nc.sync.dma_start(out=view[:, blocks, :], in_=res[h % 2][:, blocks, :])

        def store_words(cols):
            words_out = out_1[0].rearrange("p m t -> p (m t)").bitcast(I32)
            nc.sync.dma_start(out=words_out[:, cols], in_=out_codes[:, cols].bitcast(I32))

        def store_scales(cols, queues):
            for quadrant in range(4):
                queues[quadrant % len(queues)].dma_start(
                    out=out_2[0, 4 * quadrant : 4 * quadrant + 4, cols].bitcast(I32),
                    in_=out_scales[32 * quadrant : 32 * quadrant + 4, cols].bitcast(I32),
                )

        def store_head_words(h, part):
            store_words(slice(h * W, (h + 1) * W))
            if h == LAST - 1:
                store_scales(slice(0, LAST * W), [nc.sync])

        def quantise_block(h, b):
            quantise("out", h, b, PACK)
            store_words(slice(h * W + b * P, h * W + (b + 1) * P))

        steps = {
            "warm": warm,
            "gain_keys": gain_keys,
            "weave": weave,
            "logits": lambda h, t: product("z", h, t, "q", "k"),
            "softcap": softcap,
            "exp": exponent,
            "square": square,
            "add_sink": add_sink,
            "invert": invert,
            "gain": gain,
            "dprob": lambda h, t: product("dp", h, t, "do", "v"),
            "weigh": weigh,
            "shift": shift,
            "centre": centre,
            "finish": finish,
            "quant_g": lambda h, half: quantise("g", h, half, 2),
            "result": lambda h, b: product("gq", h, b, "g", "qi"),
            "scale": lambda h, b: scale_into(res[h % 2][:, b, :], last_read_of(("gq", h, b)), h),
            "round": lambda h, b: nc.scalar.copy(out=res16[:, b, :], in_=res[h % 2][:, b, :]),
            "store": lambda h, half: store(h, PAIRS[half]),
            "store_words": store_head_words,
            "quant_g_block": lambda h, b: quantise("g", h, b, PACK),
            "scale16_last": lambda h, part: scale_into(res16[:, PACK - 1, :], filled["gq", h, PACK - 1], h),
            "store_block": lambda h, b: store(h, slice(b, b + 1)),
            "turn_block": lambda h, b: turn("out", h, [b], b),
            "take_block": lambda h, b: take("out", h, P, b, "scalar"),
            "vtake_block": lambda h, b: take("out", h, P, b, "vector"),
            "quant_block": quantise_block,
            "store_scales": lambda h, part: store_scales(slice(h * W, (h + 1) * W), [nc.sync, nc.scalar]),
        }

        def operand_steps(name):
            return {
                "turn_" + name: lambda h, half: turn(name, h, [2 * half, 2 * half + 1], half),
                "take_" + name: lambda h, half: take(name, h, W // 2, half, "scalar"),
                "vtake_" + name: lambda h, half: take(name, h, W // 2, half, "vector"),
                "quant_" + name: lambda h, part: quantise(name, h, 0, 1),
                "hquant_" + name: lambda h, half: quantise(name, h, half, 2),
            }

        tables = [steps] + [operand_steps(name) for name in ("q", "k", "do", "v", "qi", "out")]
        parts_done = {}

        def run(name, h):
            family = name.replace("vtake", "take").replace("hquant", "quant")
            part = parts_done.get((family, h), 0)
            parts_done[family, h] = part + 1
            [table for table in tables if name in table][0][name](h, part)

        def tokens(text):
            return [(token.split(":")[0], int(token.split(":")[1])) for token in text.split()]

        a_view = a.rearrange("h (p t) -> p h t", t=PACK)
        nc.scalar.dma_start(out=a_first[:], in_=a_view[:, 0:1, :])
        nc.scalar.dma_start(out=sink16[:], in_=sink.partition_broadcast(P))
        load("k", k, 0, PAIRS[0])
        load("k", k, 0, PAIRS[1])
        load("q", q, 0, PAIRS[0])
        nc.sync.dma_start(out=tau16[:], in_=tau.rearrange("h (p t) -> p h t", t=PACK))
        load("do", d_o, 0, PAIRS[0])
        load("q", q, 0, PAIRS[1])
        load("do", d_o, 0, PAIRS[1])
        load("v", v, 0, PAIRS[0])
        load("v", v, 0, PAIRS[1])
        nc.sync.dma_start(out=a_rest[:], in_=a_view[:, 1:H, :])
        for h in range(1, H):
            if h == LAST:
                nc.sync.dma_start(
                    out=a_free[:].rearrange("p h d -> p (h d)"), in_=a.rearrange("h d -> (h d)").partition_broadcast(P)
                )
            for name, src in (("k", k), ("q", q), ("do", d_o), ("v", v)):
                load(name, src, h, slice(0, PACK))

        make_identity(nc, ident16[:])
        make_identity(nc, ident32[:])
        nc.gpsimd.tensor_copy(
            out=shuffle32[:].rearrange("p (c n) -> p c n", n=PACK), in_=ident32[:].rearrange("p (n c) -> p c n", n=PACK)
        )
        nc.gpsimd.tensor_scalar(out=neg_max[:], in0=sink16[:], scalar1=CAP, scalar2=-1.0, op0=ALU.max, op1=ALU.mult)
        nc.gpsimd.tensor_tensor(out=sink_gap[:], in0=sink16[:], in1=neg_max[:], op=ALU.add)
        nc.gpsimd.tensor_scalar(
            out=z_scale[:], in0=tau16[:], scalar1=inv_root_d / CAP, scalar2=0.0, op0=ALU.mult, op1=ALU.add
        )
        nc.gpsimd.tensor_copy(out=tau32[:], in_=tau16[:])
        nc.scalar.activation(out=sink_exp[:], in_=sink_gap[:], func=ACT.Exp)

        for name, h in tokens(OPENING):
            run(name, h)
        done_early = dict(parts_done)
        for period in range(H + 1):
            for name, ahead in tokens(STEADY):
                h = period + ahead
                if h < 0 or h > LAST or (h == LAST and name in CLOSING_STEPS):
                    continue
                if name != "warm" and done_early.get((name, h), 0) > 0:
                    done_early[name, h] = done_early[name, h] - 1
                    continue
                run(name, h)
        for name, h in tokens(CLOSING):
            run(name, h)
